import numpy as np
import ml_dtypes


def mxq(x, axis, fmt="e4m3"):
    dtype, down = {"e4m3": (ml_dtypes.float8_e4m3fn, 7), "e5m2": (ml_dtypes.float8_e5m2, 14)}[fmt]
    v = np.moveaxis(np.asarray(x, np.float32).astype(ml_dtypes.bfloat16).astype(np.float64), axis, -1)
    blocks = v.reshape(v.shape[:-1] + (-1, 32))
    amax = np.abs(blocks).max(-1, keepdims=True)
    byte = np.maximum(np.where(amax > 0, np.frexp(amax)[1] - 1 + 127, 0) - down, 1)
    scale = np.exp2(byte - 127.0)
    codes = (blocks / scale).astype(np.float32).astype(dtype).astype(np.float64)
    return np.moveaxis((codes * scale).reshape(v.shape), -1, axis)


WIDE = False


def mx_kscale(k):
    if not WIDE:
        return np.ones(k)
    levels = np.array([10, -10, 5, -5, 0])
    if k % 512:
        return np.exp2(np.random.permutation(np.resize(levels, k // 32))).repeat(32)
    a = np.empty((k // 512, 16))
    for p in range(k // 512):
        a[p, :8] = np.random.permutation(np.resize(levels, 8))
        for g in range(8):
            far = levels[np.abs(levels - a[p, g]) >= 10]
            a[p, g + 8] = far[np.random.randint(len(far))]
    return np.exp2(a.ravel()).repeat(32)


def f64(x):
    return np.asarray(x).astype(np.float64)


def striped(idx):
    return np.tile(idx.reshape(-1, 16).T, (8, 1)).astype(np.uint16)


def unstriped(offs):
    return offs[:16].T.reshape(-1).astype(np.int64)


E2M1 = np.array([0.0, 0.5, 1.0, 1.5, 2.0, 3.0, 4.0, 6.0, -0.0, -0.5, -1.0, -1.5, -2.0, -3.0, -4.0, -6.0])


def pack_weight(w, fmt):
    k, n = w.shape
    w = f64(np.asarray(w, np.float32).astype(ml_dtypes.bfloat16)).reshape(k // 32, 32, n)
    amax = np.abs(w).max(1)
    if fmt == "e4m3":
        byte = np.frexp(amax)[1] - 1 + 127 - 7
    else:
        mant, ex = np.frexp(amax / 6.0)
        byte = np.where(mant > 0.5, ex, ex - 1) + 127
    byte = np.clip(np.where(amax > 0, byte, 1), 1, 254)
    scaled = (w * np.exp2(127.0 - byte)[:, None, :]).reshape(k, n).astype(np.float32)
    by_word = np.ascontiguousarray(scaled.reshape(k // 512, 128, 4, n).transpose(0, 1, 3, 2))
    if fmt == "e4m3":
        words = by_word.astype(ml_dtypes.float8_e4m3fn).view(np.uint8)
    else:
        c = by_word.astype(ml_dtypes.float4_e2m1fn).view(np.uint8) & 0xF
        words = (c[..., 0::2] | (c[..., 1::2] << 4)).reshape(k // 512, 128, 2 * n)
    return np.ascontiguousarray(words), np.ascontiguousarray(byte.astype(np.uint8).reshape(k // 512, 16, n))


def unpack_weight(words, scales, fmt):
    g, _, n = scales.shape
    words = np.ascontiguousarray(words).reshape(g, 128, n, -1)
    if fmt == "e4m3":
        vals = words.view(ml_dtypes.float8_e4m3fn).astype(np.float64)
    else:
        nib = np.empty((g, 128, n, 4), np.uint8)
        nib[..., 0::2] = words & 0xF
        nib[..., 1::2] = words >> 4
        vals = E2M1[nib]
    vals = vals * np.repeat(np.exp2(scales.astype(np.float64) - 127.0), 8, axis=1)[..., None]
    return vals.transpose(0, 1, 3, 2).reshape(g * 512, n)


def relu2(v):
    return np.maximum(v, 0.0) ** 2


K, T, E, C, H, N = 2048, 640, 8, 128, 512, 512
R = 2


def by_expert(wq, xq):
    return np.concatenate([wq[e].T @ xq[:, e * C:(e + 1) * C] for e in range(E)], axis=1)


def setup_inputs():
    n = np.random.standard_normal
    s = mx_kscale(K)[:, None]
    u = mx_kscale(H)
    slot_token = np.concatenate([r * (T // R) + np.random.permutation(T // R)[:C // R] for e in range(E) for r in range(R)])
    x = pack_weight(n((K, T)) * s, "e4m3")
    return {
        "x_words": x[0],
        "x_scales": x[1],
        "w1": (n((E, K, H)) / np.sqrt(K) / s[None] * u[None, None, :]).astype(np.float32),
        "w2": (n((E, H, N)) / np.sqrt(H) / u[None, :, None] ** 2).astype(np.float32),
        "offs": striped(slot_token),
    }


def reference(x_words, x_scales, w1, w2, offs):
    idx = unstriped(offs)
    xq = unpack_weight(x_words, x_scales, "e4m3")[:, idx]
    h = relu2(by_expert(mxq(f64(w1), 1, "e4m3"), xq))
    y = by_expert(mxq(f64(w2), 1, "e4m3"), mxq(h, 0, "e4m3"))
    return y.reshape(N, E, R, C // R).transpose(0, 2, 1, 3).reshape(N, E * C)

@@ -1,0 +1,151 @@
+from contextlib import ExitStack
+
+import concourse.mybir as mybir
+from concourse.masks import make_identity
+
+K, T, E, C, H, N = 2048, 640, 8, 128, 512, 512
+R = 2
+FLOPS = 2 * E * C * (K * H + H * N)
+
+F32 = mybir.dt.float32
+BF16 = mybir.dt.bfloat16
+I32 = mybir.dt.int32
+U32 = mybir.dt.uint32
+U16 = mybir.dt.uint16
+U8 = mybir.dt.uint8
+FP8X4 = mybir.dt.float8_e4m3fn_x4
+ACT = mybir.ActivationFunctionType
+
+P = 128
+PACK = 4
+K_PASS = P * PACK
+PASSES = K // K_PASS
+PAIR = 2
+U = C // R
+CHUNKS = N // P
+RAW_BUFS = 8
+BULK = E - PAIR
+
+
+def tile_moe_pke_mlp_relu2_kernel(tc, x_words, x_scales, w1, w2, offs, out):
+    nc = tc.nc
+    with ExitStack() as ctx:
+        keep = ctx.enter_context(tc.tile_pool(name="keep", bufs=1))
+        raws = ctx.enter_context(tc.tile_pool(name="raws", bufs=RAW_BUFS))
+        work = ctx.enter_context(tc.tile_pool(name="work", bufs=2))
+        psum = ctx.enter_context(tc.psum_pool(name="psum", bufs=2))
+
+        offsets = keep.tile([P, E * C // 16], U16, name="offsets")
+        nc.sync.dma_start(offsets[:], offs)
+        tok_words = keep.tile([P, PASSES * T], U32, name="tok_words", align_bytes=64)
+        nc.sync.dma_start(
+            tok_words[:].bitcast(I32).rearrange("p (o t) -> p o t", o=PASSES),
+            x_words.rearrange("o p t r -> p o (t r)").bitcast(I32),
+        )
+        tok_scales = keep.tile([P, T], U8, name="tok_scales", align_bytes=64)
+        nc.vector.memset(tok_scales[:].bitcast(I32), 0)
+        for q in range(4):
+            nc.sync.dma_start(
+                tok_scales[32 * q : 32 * q + 16, :].bitcast(I32),
+                x_scales[:, 4 * q : 4 * q + 4, :].bitcast(I32),
+            )
+        ident = keep.tile([P, P], F32, name="ident")
+        make_identity(nc, ident[:])
+        y_bulk = keep.tile([P, CHUNKS, R, BULK * U], F32, name="y_bulk")
+        y_last = keep.tile([P, CHUNKS, R, PAIR * U], F32, name="y_last")
+
+        def load(src, blocks, width):
+            raw = raws.tile([P, blocks, PACK, width], F32, name="raw")
+            nc.sync.dma_start(raw[:], src.rearrange("(a p j) n -> p a j n", a=blocks, j=PACK))
+            return raw
+
+        def quantise(raw_block, width, tag, bufs):
+            grouped = work.tile([P, width * PACK], BF16, name="grouped", bufs=4, align_bytes=64)
+            src = raw_block.rearrange("p j (c i) -> p c j i", i=4)
+            dst = grouped[:].rearrange("p (c i j) -> p c j i", i=4, j=PACK)
+            half = width // 8
+            nc.vector.tensor_copy(dst[:, :half, :, :], src[:, :half, :, :])
+            nc.scalar.copy(dst[:, half:, :, :], src[:, half:, :, :])
+            codes = work.tile([P, width], U32, name=tag + "_codes", bufs=bufs, align_bytes=64)
+            scales = work.tile([P, width], U8, name=tag + "_scales", bufs=bufs, align_bytes=64)
+            nc.vector.quantize_mx(codes[:].bitcast(FP8X4), scales[:], grouped[:])
+            return codes, scales
+
+        def gather(pair):
+            lst = offsets[:, pair * PAIR * C // 16 : (pair + 1) * PAIR * C // 16]
+            words = work.tile([P, PASSES, PAIR * C], U32, name="slot_words", align_bytes=64)
+            for o in range(PASSES):
+                nc.vector.tensor_copy(words[:, o, :], tok_words[:, o * T : (o + 1) * T].indirect(lst))
+            scales = work.tile([P, PAIR * C], U8, name="slot_scales", align_bytes=64)
+            nc.vector.tensor_copy(scales[:], tok_scales[:].indirect(lst))
+            return words, scales
+
+        def layer1(e, slot_words, slot_scales):
+            slots = slice((e % PAIR) * C, (e % PAIR + 1) * C)
+            acc = psum.tile([P, H], F32, name="acc")
+            for g in range(PASSES // 2):
+                raw = load(w1[e, 2 * g * K_PASS : 2 * (g + 1) * K_PASS, :], 2, H)
+                for a in range(2):
+                    o = 2 * g + a
+                    codes, scales = quantise(raw[:, a, :, :], H, "w1", 6)
+                    nc.tensor.matmul_mx(
+                        out=acc[:],
+                        lhsT=slot_words[:, o, slots].bitcast(FP8X4),
+                        lhsT_scale=slot_scales[4 * o :, slots],
+                        rhs=codes[:].bitcast(FP8X4),
+                        rhs_scale=scales[:],
+                        start=(o == 0),
+                        stop=(o == PASSES - 1),
+                    )
+            relu = work.tile([P, PACK, P], F32, name="relu")
+            nc.scalar.activation(relu[:], acc[:].rearrange("s (m t) -> s t m", t=PACK), ACT.Relu)
+            turned = psum.tile([P, PACK, C], F32, name="turned")
+            for t in range(PACK):
+                nc.tensor.transpose(turned[:, t, :], relu[:, t, :], ident[:])
+            h_bf = work.tile([P, C * PACK], BF16, name="h_bf", align_bytes=64)
+            nc.scalar.activation(
+                h_bf[:].rearrange("m (s t) -> m s t", t=PACK), turned[:].rearrange("m t s -> m s t"), ACT.Square
+            )
+            h_codes = work.tile([P, C], U32, name="h_codes", bufs=4, align_bytes=64)
+            h_scales = work.tile([P, C], U8, name="h_scales", bufs=4, align_bytes=64)
+            nc.vector.quantize_mx(h_codes[:].bitcast(FP8X4), h_scales[:], h_bf[:])
+            return h_codes, h_scales
+
+        def layer2(e, raw_block, c0, chunks, h):
+            codes, scales = quantise(raw_block, chunks * P, "w2", 3)
+            y = psum.tile([P, chunks, C], F32, name="y")
+            for c in range(chunks):
+                nc.tensor.matmul_mx(
+                    out=y[:, c, :],
+                    lhsT=codes[:, c * P : (c + 1) * P].bitcast(FP8X4),
+                    lhsT_scale=scales[:, c * P : (c + 1) * P],
+                    rhs=h[0][:].bitcast(FP8X4),
+                    rhs_scale=h[1][:],
+                    start=True,
+                    stop=True,
+                )
+            stage, place = (y_bulk, e) if e < BULK else (y_last, e - BULK)
+            nc.scalar.copy(
+                stage[:, c0 : c0 + chunks, :, place * U : (place + 1) * U],
+                y[:].rearrange("p c (m u) -> p c m u", m=R),
+            )
+
+        out_v = out.rearrange("(c p) (m x) -> p c m x", p=P, m=R)
+        for pair in range(E // PAIR):
+            slot_words, slot_scales = gather(pair)
+            experts = range(pair * PAIR, (pair + 1) * PAIR)
+            hs = [layer1(e, slot_words, slot_scales) for e in experts]
+            if pair * PAIR < BULK:
+                raw = load(w2[pair * PAIR : (pair + 1) * PAIR].rearrange("e i n -> (e i) n"), PAIR, N)
+                for a, e in enumerate(experts):
+                    layer2(e, raw[:, a, :, :], 0, CHUNKS, hs[a])
+            else:
+                raw = load(w2[E - 2], 1, N)
+                halves = [load(w2[E - 1, :, b * N // 2 : (b + 1) * N // 2], 1, N // 2) for b in range(2)]
+                for m in range(R):
+                    nc.sync.dma_start(out_v[:, :, m, : BULK * U], y_bulk[:, :, m, :])
+                layer2(E - 2, raw[:, 0, :, :], 0, CHUNKS, hs[0])
+                for b in range(2):
+                    layer2(E - 1, halves[b][:, 0, :, :], 2 * b, 2, hs[1])
+                    for c in range(2 * b, 2 * b + 2):
+                        nc.sync.dma_start(out_v[:, c, :, BULK * U :], y_last[:, c, :, :])

@@ -24,7 +24,8 @@ PAIR = 2
 U = C // R
 CHUNKS = N // P
 RAW_BUFS = 8
-BULK = E - PAIR
+LAG = 3
+STORE_GROUPS = (range(0, 5), range(5, 7), range(7, 8))
 
 
 def tile_moe_pke_mlp_relu2_kernel(tc, x_words, x_scales, w1, w2, offs, out):
@@ -51,21 +52,26 @@ def tile_moe_pke_mlp_relu2_kernel(tc, x_words, x_scales, w1, w2, offs, out):
             )
         ident = keep.tile([P, P], F32, name="ident")
         make_identity(nc, ident[:])
-        y_bulk = keep.tile([P, CHUNKS, R, BULK * U], F32, name="y_bulk")
-        y_last = keep.tile([P, CHUNKS, R, PAIR * U], F32, name="y_last")
+        staged = [keep.tile([P, CHUNKS, R, len(g) * U], F32, name=f"staged{g.start}") for g in STORE_GROUPS]
 
-        def load(src, blocks, width):
-            raw = raws.tile([P, blocks, PACK, width], F32, name="raw")
-            nc.sync.dma_start(raw[:], src.rearrange("(a p j) n -> p a j n", a=blocks, j=PACK))
+        def load(rows, blocks):
+            raw = raws.tile([P, blocks, PACK, rows.shape[1]], F32, name="raw")
+            nc.sync.dma_start(raw[:], rows.rearrange("(a p j) n -> p a j n", a=blocks, j=PACK))
             return raw
 
-        def quantise(raw_block, width, tag, bufs):
+        def interleave(block, share):
+            width = block.shape[2]
             grouped = work.tile([P, width * PACK], BF16, name="grouped", bufs=4, align_bytes=64)
-            src = raw_block.rearrange("p j (c i) -> p c j i", i=4)
+            src = block.rearrange("p j (c i) -> p c j i", i=4)
             dst = grouped[:].rearrange("p (c i j) -> p c j i", i=4, j=PACK)
-            half = width // 8
-            nc.vector.tensor_copy(dst[:, :half, :, :], src[:, :half, :, :])
-            nc.scalar.copy(dst[:, half:, :, :], src[:, half:, :, :])
+            cut = width // 4 * share // 16
+            nc.vector.tensor_copy(dst[:, :cut, :, :], src[:, :cut, :, :])
+            if share < 16:
+                nc.scalar.copy(dst[:, cut:, :, :], src[:, cut:, :, :])
+            return grouped
+
+        def quantise(grouped, tag, bufs):
+            width = grouped.shape[1] // PACK
             codes = work.tile([P, width], U32, name=tag + "_codes", bufs=bufs, align_bytes=64)
             scales = work.tile([P, width], U8, name=tag + "_scales", bufs=bufs, align_bytes=64)
             nc.vector.quantize_mx(codes[:].bitcast(FP8X4), scales[:], grouped[:])
@@ -73,24 +79,26 @@ def tile_moe_pke_mlp_relu2_kernel(tc, x_words, x_scales, w1, w2, offs, out):
 
         def gather(pair):
             lst = offsets[:, pair * PAIR * C // 16 : (pair + 1) * PAIR * C // 16]
-            words = work.tile([P, PASSES, PAIR * C], U32, name="slot_words", align_bytes=64)
-            for o in range(PASSES):
-                nc.vector.tensor_copy(words[:, o, :], tok_words[:, o * T : (o + 1) * T].indirect(lst))
             scales = work.tile([P, PAIR * C], U8, name="slot_scales", align_bytes=64)
             nc.vector.tensor_copy(scales[:], tok_scales[:].indirect(lst))
+            words = []
+            for o in range(PASSES):
+                words.append(work.tile([P, PAIR * C], U32, name="slot_words", bufs=PASSES + 1, align_bytes=64))
+                nc.vector.tensor_copy(words[o][:], tok_words[:, o * T : (o + 1) * T].indirect(lst))
             return words, scales
 
         def layer1(e, slot_words, slot_scales):
             slots = slice((e % PAIR) * C, (e % PAIR + 1) * C)
             acc = psum.tile([P, H], F32, name="acc")
             for g in range(PASSES // 2):
-                raw = load(w1[e, 2 * g * K_PASS : 2 * (g + 1) * K_PASS, :], 2, H)
+                raw = load(w1[e, 2 * g * K_PASS : 2 * (g + 1) * K_PASS, :], 2)
+                grouped = [interleave(raw[:, a, :, :], 8) for a in range(2)]
                 for a in range(2):
                     o = 2 * g + a
-                    codes, scales = quantise(raw[:, a, :, :], H, "w1", 6)
+                    codes, scales = quantise(grouped[a], "w1", 8)
                     nc.tensor.matmul_mx(
                         out=acc[:],
-                        lhsT=slot_words[:, o, slots].bitcast(FP8X4),
+                        lhsT=slot_words[o][:, slots].bitcast(FP8X4),
                         lhsT_scale=slot_scales[4 * o :, slots],
                         rhs=codes[:].bitcast(FP8X4),
                         rhs_scale=scales[:],
@@ -106,13 +114,11 @@ def tile_moe_pke_mlp_relu2_kernel(tc, x_words, x_scales, w1, w2, offs, out):
             nc.scalar.activation(
                 h_bf[:].rearrange("m (s t) -> m s t", t=PACK), turned[:].rearrange("m t s -> m s t"), ACT.Square
             )
-            h_codes = work.tile([P, C], U32, name="h_codes", bufs=4, align_bytes=64)
-            h_scales = work.tile([P, C], U8, name="h_scales", bufs=4, align_bytes=64)
-            nc.vector.quantize_mx(h_codes[:].bitcast(FP8X4), h_scales[:], h_bf[:])
-            return h_codes, h_scales
+            return quantise(h_bf, "h", LAG + 2) if e < E - 2 else quantise(h_bf, "h6", 1) if e == E - 2 else h_bf
 
-        def layer2(e, raw_block, c0, chunks, h):
-            codes, scales = quantise(raw_block, chunks * P, "w2", 3)
+        def layer2(e, c0, chunks, h):
+            raw = load(w2[e, :, c0 * P : (c0 + chunks) * P], 1)
+            codes, scales = quantise(interleave(raw[:, 0, :, :], 10 if e < E - LAG else 4 if (e, c0) == (E - 1, 0) else 16), "w2", 3)
             y = psum.tile([P, chunks, C], F32, name="y")
             for c in range(chunks):
                 nc.tensor.matmul_mx(
@@ -124,28 +130,33 @@ def tile_moe_pke_mlp_relu2_kernel(tc, x_words, x_scales, w1, w2, offs, out):
                     start=True,
                     stop=True,
                 )
-            stage, place = (y_bulk, e) if e < BULK else (y_last, e - BULK)
-            nc.scalar.copy(
+            g = [e in group for group in STORE_GROUPS].index(True)
+            stage, place = staged[g], e - STORE_GROUPS[g].start
+            copy = nc.vector.tensor_copy if c0 > 0 else nc.scalar.copy
+            copy(
                 stage[:, c0 : c0 + chunks, :, place * U : (place + 1) * U],
                 y[:].rearrange("p c (m u) -> p c m u", m=R),
             )
 
         out_v = out.rearrange("(c p) (m x) -> p c m x", p=P, m=R)
-        for pair in range(E // PAIR):
-            slot_words, slot_scales = gather(pair)
-            experts = range(pair * PAIR, (pair + 1) * PAIR)
-            hs = [layer1(e, slot_words, slot_scales) for e in experts]
-            if pair * PAIR < BULK:
-                raw = load(w2[pair * PAIR : (pair + 1) * PAIR].rearrange("e i n -> (e i) n"), PAIR, N)
-                for a, e in enumerate(experts):
-                    layer2(e, raw[:, a, :, :], 0, CHUNKS, hs[a])
-            else:
-                raw = load(w2[E - 2], 1, N)
-                halves = [load(w2[E - 1, :, b * N // 2 : (b + 1) * N // 2], 1, N // 2) for b in range(2)]
+        hs = []
+        for step in range(E + LAG):
+            if step < E:
+                if step % PAIR == 0:
+                    slot_words, slot_scales = gather(step // PAIR)
+                hs.append(layer1(step, slot_words, slot_scales))
+            e = step - LAG
+            if e >= 0:
+                h = hs[e]
+                if e < E - 1:
+                    layer2(e, 0, CHUNKS, h)
+                else:
+                    h = quantise(h, "h6", 1)
+                    for b in range(2):
+                        layer2(e, 2 * b, 2, h)
+        for group, stage in zip(STORE_GROUPS, staged):
+            cols = slice(group.start * U, group.stop * U)
+            pieces = (slice(0, 2), slice(2, 4)) if group.stop == E else (slice(0, CHUNKS),)
+            for cs in pieces:
                 for m in range(R):
-                    nc.sync.dma_start(out_v[:, :, m, : BULK * U], y_bulk[:, :, m, :])
-                layer2(E - 2, raw[:, 0, :, :], 0, CHUNKS, hs[0])
-                for b in range(2):
-                    layer2(E - 1, halves[b][:, 0, :, :], 2 * b, 2, hs[1])
-                    for c in range(2 * b, 2 * b + 2):
-                        nc.sync.dma_start(out_v[:, c, :, BULK * U :], y_last[:, c, :, :])
+                    nc.sync.dma_start(out_v[:, cs, m, cols], stage[:, cs, m, :])

@@ -23,7 +23,7 @@ PASSES = K // K_PASS
 PAIR = 2
 U = C // R
 CHUNKS = N // P
-RAW_BUFS = 8
+RAW_BUFS = 4
 LAG = 3
 STORE_GROUPS = (range(0, 5), range(5, 7), range(7, 8))
 
@@ -44,7 +44,7 @@ def tile_moe_pke_mlp_relu2_kernel(tc, x_words, x_scales, w1, w2, offs, out):
             x_words.rearrange("o p t r -> p o (t r)").bitcast(I32),
         )
         tok_scales = keep.tile([P, T], U8, name="tok_scales", align_bytes=64)
-        nc.vector.memset(tok_scales[:].bitcast(I32), 0)
+        nc.gpsimd.memset(tok_scales[:].bitcast(I32), 0)
         for q in range(4):
             nc.sync.dma_start(
                 tok_scales[32 * q : 32 * q + 16, :].bitcast(I32),
@@ -90,9 +90,11 @@ def tile_moe_pke_mlp_relu2_kernel(tc, x_words, x_scales, w1, w2, offs, out):
         def layer1(e, slot_words, slot_scales):
             slots = slice((e % PAIR) * C, (e % PAIR + 1) * C)
             acc = psum.tile([P, H], F32, name="acc")
+            blocks = PASSES if e < E - 1 else 2
             for g in range(PASSES // 2):
-                raw = load(w1[e, 2 * g * K_PASS : 2 * (g + 1) * K_PASS, :], 2)
-                grouped = [interleave(raw[:, a, :, :], 8) for a in range(2)]
+                if 2 * g % blocks == 0:
+                    raw = load(w1[e, 2 * g * K_PASS : (2 * g + blocks) * K_PASS, :], blocks)
+                grouped = [interleave(raw[:, (2 * g + a) % blocks, :, :], 8) for a in range(2)]
                 for a in range(2):
                     o = 2 * g + a
                     codes, scales = quantise(grouped[a], "w1", 8)

from contextlib import ExitStack

import concourse.mybir as mybir
from concourse.masks import make_identity

K, T, E, C, H, N = 2048, 640, 8, 128, 512, 512
R = 2
FLOPS = 2 * E * C * (K * H + H * N)

F32 = mybir.dt.float32
BF16 = mybir.dt.bfloat16
I32 = mybir.dt.int32
U32 = mybir.dt.uint32
U16 = mybir.dt.uint16
U8 = mybir.dt.uint8
FP8X4 = mybir.dt.float8_e4m3fn_x4
ACT = mybir.ActivationFunctionType

P = 128
PACK = 4
K_PASS = P * PACK
PASSES = K // K_PASS
PAIR = 2
U = C // R
CHUNKS = N // P
RAW_BUFS = 4
LAG = 3
STORE_GROUPS = (range(0, 5), range(5, 7), range(7, 8))


def tile_moe_pke_mlp_relu2_kernel(tc, x_words, x_scales, w1, w2, offs, out):
    nc = tc.nc
    with ExitStack() as ctx:
        keep = ctx.enter_context(tc.tile_pool(name="keep", bufs=1))
        raws = ctx.enter_context(tc.tile_pool(name="raws", bufs=RAW_BUFS))
        work = ctx.enter_context(tc.tile_pool(name="work", bufs=2))
        psum = ctx.enter_context(tc.psum_pool(name="psum", bufs=2))

        offsets = keep.tile([P, E * C // 16], U16, name="offsets")
        nc.sync.dma_start(offsets[:], offs)
        tok_words = keep.tile([P, PASSES * T], U32, name="tok_words", align_bytes=64)
        nc.sync.dma_start(
            tok_words[:].bitcast(I32).rearrange("p (o t) -> p o t", o=PASSES),
            x_words.rearrange("o p t r -> p o (t r)").bitcast(I32),
        )
        tok_scales = keep.tile([P, T], U8, name="tok_scales", align_bytes=64)
        nc.gpsimd.memset(tok_scales[:].bitcast(I32), 0)
        for q in range(4):
            nc.sync.dma_start(
                tok_scales[32 * q : 32 * q + 16, :].bitcast(I32),
                x_scales[:, 4 * q : 4 * q + 4, :].bitcast(I32),
            )
        ident = keep.tile([P, P], F32, name="ident")
        make_identity(nc, ident[:])
        staged = [keep.tile([P, CHUNKS, R, len(g) * U], F32, name=f"staged{g.start}") for g in STORE_GROUPS]

        def load(rows, blocks):
            raw = raws.tile([P, blocks, PACK, rows.shape[1]], F32, name="raw")
            nc.sync.dma_start(raw[:], rows.rearrange("(a p j) n -> p a j n", a=blocks, j=PACK))
            return raw

        def interleave(block, share):
            width = block.shape[2]
            grouped = work.tile([P, width * PACK], BF16, name="grouped", bufs=4, align_bytes=64)
            src = block.rearrange("p j (c i) -> p c j i", i=4)
            dst = grouped[:].rearrange("p (c i j) -> p c j i", i=4, j=PACK)
            cut = width // 4 * share // 16
            nc.vector.tensor_copy(dst[:, :cut, :, :], src[:, :cut, :, :])
            if share < 16:
                nc.scalar.copy(dst[:, cut:, :, :], src[:, cut:, :, :])
            return grouped

        def quantise(grouped, tag, bufs):
            width = grouped.shape[1] // PACK
            codes = work.tile([P, width], U32, name=tag + "_codes", bufs=bufs, align_bytes=64)
            scales = work.tile([P, width], U8, name=tag + "_scales", bufs=bufs, align_bytes=64)
            nc.vector.quantize_mx(codes[:].bitcast(FP8X4), scales[:], grouped[:])
            return codes, scales

        def gather(pair):
            lst = offsets[:, pair * PAIR * C // 16 : (pair + 1) * PAIR * C // 16]
            scales = work.tile([P, PAIR * C], U8, name="slot_scales", align_bytes=64)
            nc.vector.tensor_copy(scales[:], tok_scales[:].indirect(lst))
            words = []
            for o in range(PASSES):
                words.append(work.tile([P, PAIR * C], U32, name="slot_words", bufs=PASSES + 1, align_bytes=64))
                nc.vector.tensor_copy(words[o][:], tok_words[:, o * T : (o + 1) * T].indirect(lst))
            return words, scales

        def layer1(e, slot_words, slot_scales):
            slots = slice((e % PAIR) * C, (e % PAIR + 1) * C)
            acc = psum.tile([P, H], F32, name="acc")
            blocks = PASSES if e < E - 1 else 2
            for g in range(PASSES // 2):
                if 2 * g % blocks == 0:
                    raw = load(w1[e, 2 * g * K_PASS : (2 * g + blocks) * K_PASS, :], blocks)
                grouped = [interleave(raw[:, (2 * g + a) % blocks, :, :], 8) for a in range(2)]
                for a in range(2):
                    o = 2 * g + a
                    codes, scales = quantise(grouped[a], "w1", 8)
                    nc.tensor.matmul_mx(
                        out=acc[:],
                        lhsT=slot_words[o][:, slots].bitcast(FP8X4),
                        lhsT_scale=slot_scales[4 * o :, slots],
                        rhs=codes[:].bitcast(FP8X4),
                        rhs_scale=scales[:],
                        start=(o == 0),
                        stop=(o == PASSES - 1),
                    )
            relu = work.tile([P, PACK, P], F32, name="relu")
            nc.scalar.activation(relu[:], acc[:].rearrange("s (m t) -> s t m", t=PACK), ACT.Relu)
            turned = psum.tile([P, PACK, C], F32, name="turned")
            for t in range(PACK):
                nc.tensor.transpose(turned[:, t, :], relu[:, t, :], ident[:])
            h_bf = work.tile([P, C * PACK], BF16, name="h_bf", align_bytes=64)
            nc.scalar.activation(
                h_bf[:].rearrange("m (s t) -> m s t", t=PACK), turned[:].rearrange("m t s -> m s t"), ACT.Square
            )
            return quantise(h_bf, "h", LAG + 2) if e < E - 2 else quantise(h_bf, "h6", 1) if e == E - 2 else h_bf

        def layer2(e, c0, chunks, h):
            raw = load(w2[e, :, c0 * P : (c0 + chunks) * P], 1)
            codes, scales = quantise(interleave(raw[:, 0, :, :], 10 if e < E - LAG else 4 if (e, c0) == (E - 1, 0) else 16), "w2", 3)
            y = psum.tile([P, chunks, C], F32, name="y")
            for c in range(chunks):
                nc.tensor.matmul_mx(
                    out=y[:, c, :],
                    lhsT=codes[:, c * P : (c + 1) * P].bitcast(FP8X4),
                    lhsT_scale=scales[:, c * P : (c + 1) * P],
                    rhs=h[0][:].bitcast(FP8X4),
                    rhs_scale=h[1][:],
                    start=True,
                    stop=True,
                )
            g = [e in group for group in STORE_GROUPS].index(True)
            stage, place = staged[g], e - STORE_GROUPS[g].start
            copy = nc.vector.tensor_copy if c0 > 0 else nc.scalar.copy
            copy(
                stage[:, c0 : c0 + chunks, :, place * U : (place + 1) * U],
                y[:].rearrange("p c (m u) -> p c m u", m=R),
            )

        out_v = out.rearrange("(c p) (m x) -> p c m x", p=P, m=R)
        hs = []
        for step in range(E + LAG):
            if step < E:
                if step % PAIR == 0:
                    slot_words, slot_scales = gather(step // PAIR)
                hs.append(layer1(step, slot_words, slot_scales))
            e = step - LAG
            if e >= 0:
                h = hs[e]
                if e < E - 1:
                    layer2(e, 0, CHUNKS, h)
                else:
                    h = quantise(h, "h6", 1)
                    for b in range(2):
                        layer2(e, 2 * b, 2, h)
        for group, stage in zip(STORE_GROUPS, staged):
            cols = slice(group.start * U, group.stop * U)
            pieces = (slice(0, 2), slice(2, 4)) if group.stop == E else (slice(0, CHUNKS),)
            for cs in pieces:
                for m in range(R):
                    nc.sync.dma_start(out_v[:, cs, m, cols], stage[:, cs, m, :])
